import numpy as np
import ml_dtypes


def mxq(x, axis, fmt="e4m3"):
    dtype, down = {"e4m3": (ml_dtypes.float8_e4m3fn, 7), "e5m2": (ml_dtypes.float8_e5m2, 14)}[fmt]
    v = np.moveaxis(np.asarray(x, np.float32).astype(ml_dtypes.bfloat16).astype(np.float64), axis, -1)
    blocks = v.reshape(v.shape[:-1] + (-1, 32))
    amax = np.abs(blocks).max(-1, keepdims=True)
    byte = np.maximum(np.where(amax > 0, np.frexp(amax)[1] - 1 + 127, 0) - down, 1)
    scale = np.exp2(byte - 127.0)
    codes = (blocks / scale).astype(np.float32).astype(dtype).astype(np.float64)
    return np.moveaxis((codes * scale).reshape(v.shape), -1, axis)


WIDE = False


def mx_kscale(k):
    if not WIDE:
        return np.ones(k)
    levels = np.array([10, -10, 5, -5, 0])
    if k % 512:
        return np.exp2(np.random.permutation(np.resize(levels, k // 32))).repeat(32)
    a = np.empty((k // 512, 16))
    for p in range(k // 512):
        a[p, :8] = np.random.permutation(np.resize(levels, 8))
        for g in range(8):
            far = levels[np.abs(levels - a[p, g]) >= 10]
            a[p, g + 8] = far[np.random.randint(len(far))]
    return np.exp2(a.ravel()).repeat(32)


def f64(x):
    return np.asarray(x).astype(np.float64)


def striped(idx):
    return np.tile(idx.reshape(-1, 16).T, (8, 1)).astype(np.uint16)


def unstriped(offs):
    return offs[:16].T.reshape(-1).astype(np.int64)


E2M1 = np.array([0.0, 0.5, 1.0, 1.5, 2.0, 3.0, 4.0, 6.0, -0.0, -0.5, -1.0, -1.5, -2.0, -3.0, -4.0, -6.0])


def pack_weight(w, fmt):
    k, n = w.shape
    w = f64(np.asarray(w, np.float32).astype(ml_dtypes.bfloat16)).reshape(k // 32, 32, n)
    amax = np.abs(w).max(1)
    if fmt == "e4m3":
        byte = np.frexp(amax)[1] - 1 + 127 - 7
    else:
        mant, ex = np.frexp(amax / 6.0)
        byte = np.where(mant > 0.5, ex, ex - 1) + 127
    byte = np.clip(np.where(amax > 0, byte, 1), 1, 254)
    scaled = (w * np.exp2(127.0 - byte)[:, None, :]).reshape(k, n).astype(np.float32)
    by_word = np.ascontiguousarray(scaled.reshape(k // 512, 128, 4, n).transpose(0, 1, 3, 2))
    if fmt == "e4m3":
        words = by_word.astype(ml_dtypes.float8_e4m3fn).view(np.uint8)
    else:
        c = by_word.astype(ml_dtypes.float4_e2m1fn).view(np.uint8) & 0xF
        words = (c[..., 0::2] | (c[..., 1::2] << 4)).reshape(k // 512, 128, 2 * n)
    return np.ascontiguousarray(words), np.ascontiguousarray(byte.astype(np.uint8).reshape(k // 512, 16, n))


def unpack_weight(words, scales, fmt):
    g, _, n = scales.shape
    words = np.ascontiguousarray(words).reshape(g, 128, n, -1)
    if fmt == "e4m3":
        vals = words.view(ml_dtypes.float8_e4m3fn).astype(np.float64)
    else:
        nib = np.empty((g, 128, n, 4), np.uint8)
        nib[..., 0::2] = words & 0xF
        nib[..., 1::2] = words >> 4
        vals = E2M1[nib]
    vals = vals * np.repeat(np.exp2(scales.astype(np.float64) - 127.0), 8, axis=1)[..., None]
    return vals.transpose(0, 1, 3, 2).reshape(g * 512, n)


def relu(v):
    return np.maximum(v, 0.0)


K, T, E, H, N = 1024, 512, 4, 512, 256
COUNTS = (128, 256, 384, 256)
STARTS = np.cumsum((0,) + COUNTS)


def by_expert(wq, xq):
    return np.concatenate([wq[e].T @ xq[:, STARTS[e]:STARTS[e + 1]] for e in range(E)], axis=1)


def setup_inputs():
    n = np.random.standard_normal
    s = mx_kscale(K)[:, None]
    u = mx_kscale(H)
    both = np.repeat(np.arange(E), COUNTS)
    pair = np.stack([both[:T], both[T:]])[:, np.random.permutation(T)]
    pair = np.where(np.random.rand(T) < 0.5, pair, pair[::-1])
    order = np.argsort(pair.reshape(-1), kind="stable")
    slot_token = order % T; pos = np.empty(2 * T, np.int64); pos[order] = np.arange(2 * T); pos = pos.reshape(2, T)
    g = np.random.uniform(0.2, 0.8, T)
    w1 = [pack_weight(m, "e2m1") for m in n((E, K, H)) / np.sqrt(K) / s[None]]
    w3 = [pack_weight(m, "e2m1") for m in n((E, K, H)) / np.sqrt(K) / s[None] * u[None, None, :]]
    w2 = [pack_weight(m, "e2m1") for m in n((E, H, N)) / np.sqrt(H) / u[None, :, None]]
    return {
        "xT": (n((K, T)) * s).astype(np.float32),
        "w1_words": np.stack([m[0] for m in w1]),
        "w1_scales": np.stack([m[1] for m in w1]),
        "w3_words": np.stack([m[0] for m in w3]),
        "w3_scales": np.stack([m[1] for m in w3]),
        "w2_words": np.stack([m[0] for m in w2]),
        "w2_scales": np.stack([m[1] for m in w2]),
        "gate": np.stack([np.tile(g, (N, 1)), np.tile(1.0 - g, (N, 1))]).astype(np.float32),
        "offs": striped(slot_token),
        "pos1": striped(pos[0]),
        "pos2": striped(pos[1]),
    }


def reference(xT, w1_words, w1_scales, w3_words, w3_scales, w2_words, w2_scales, gate, offs, pos1, pos2):
    idx = unstriped(offs)
    w1 = np.stack([unpack_weight(w1_words[e], w1_scales[e], "e2m1") for e in range(E)])
    w3 = np.stack([unpack_weight(w3_words[e], w3_scales[e], "e2m1") for e in range(E)])
    w2 = np.stack([unpack_weight(w2_words[e], w2_scales[e], "e2m1") for e in range(E)])
    xq = mxq(f64(xT)[:, idx], 0, "e4m3")
    h = relu(by_expert(w1, xq))
    h = h * by_expert(w3, xq)
    y = by_expert(w2, mxq(h, 0, "e4m3"))
    return f64(gate[0]) * y[:, unstriped(pos1)] + f64(gate[1]) * y[:, unstriped(pos2)]

from contextlib import ExitStack

import concourse.mybir as mybir
from concourse.masks import make_identity

K, T, E, H, N = 1024, 512, 4, 512, 256
S = 2 * T
FLOPS = 2 * S * (2 * K * H + H * N)
BYTES = 4 * K * T + 2 * (E * K * H // 2 + E * K * H // 32) + E * H * N // 2 + E * H * N // 32 + 4 * N * T + 4 * 2 * T

F32 = mybir.dt.float32
BF16 = mybir.dt.bfloat16
I32 = mybir.dt.int32
U32 = mybir.dt.uint32
U16 = mybir.dt.uint16
U8 = mybir.dt.uint8
E4M3 = mybir.dt.float8_e4m3fn_x4
E2M1 = mybir.dt.float4_e2m1fn_x4
MULT = mybir.AluOpType.mult
ADD = mybir.AluOpType.add
COPY = mybir.ActivationFunctionType.Copy
RELU = mybir.ActivationFunctionType.Relu

PIECES = ((2, 384, 128), (2, 512, 256), (3, 768, 256), (1, 128, 256), (0, 0, 128))


def tile_moe_rag_glu_relu_kernel(
    tc, xT, w1_words, w1_scales, w3_words, w3_scales, w2_words, w2_scales, gate, offs, pos1, pos2, out
):
    nc = tc.nc
    with ExitStack() as ctx:
        lists = ctx.enter_context(tc.tile_pool(name="lists", bufs=1))
        keep = ctx.enter_context(tc.tile_pool(name="keep", bufs=1))
        psum = ctx.enter_context(tc.psum_pool(name="psum", bufs=2))

        offs_t = lists.tile([128, S // 16], U16, name="offs_t")
        pos1_t = lists.tile([128, T // 16], U16, name="pos1_t")
        pos2_t = lists.tile([128, T // 16], U16, name="pos2_t")

        raw = {}
        grouped = {}
        for s in range(2):
            for c in range(2):
                raw[s, c] = keep.tile([128, 4, 256], F32, name=f"raw{s}{c}")
                grouped[s, c] = keep.tile([128, 256, 4], BF16, name=f"grouped{s}{c}", align_bytes=64)
        codes = [keep.tile([128, T], U32, name=f"codes{s}", align_bytes=64) for s in range(2)]
        bytes_ = [keep.tile([128, T], U8, name=f"scales{s}", align_bytes=64) for s in range(2)]
        g_codes = [keep.tile([128, S], U32, name=f"g_codes{s}", align_bytes=64) for s in range(2)]
        g_bytes = [keep.tile([128, S], U8, name=f"g_scales{s}", align_bytes=64) for s in range(2)]
        words = {1: keep.tile([128, E * 2 * 1024], U8, name="w1_t", align_bytes=64),
                 3: keep.tile([128, E * 2 * 1024], U8, name="w3_t", align_bytes=64)}
        planes = {1: keep.tile([128, E * 2 * 512], U8, name="w1_plane", align_bytes=64),
                  3: keep.tile([128, E * 2 * 512], U8, name="w3_plane", align_bytes=64)}
        w2_t = keep.tile([128, E * 512], U8, name="w2_t", align_bytes=64)
        w2_plane = keep.tile([128, E * 256], U8, name="w2_plane", align_bytes=64)
        gates = [keep.tile([128, T], F32, name=f"gate{g}") for g in range(2)]
        y = [keep.tile([128, S], F32, name=f"y{n}") for n in range(2)]
        ident = keep.tile([128, 128], F32, name="ident")
        warm = keep.tile([128, 1], F32, name="warm")

        nc.vector.memset(warm[:], 0.0)
        nc.scalar.activation(warm[:], warm[:], RELU)
        for w in (1, 3):
            nc.vector.memset(planes[w][:].bitcast(I32), 0)
        for s in range(2):
            nc.vector.memset(bytes_[s][:].bitcast(I32), 0)
        nc.vector.memset(w2_plane[:].bitcast(I32), 0)

        word_src = {1: w1_words.bitcast(I32), 3: w3_words.bitcast(I32)}
        scale_src = {1: w1_scales.bitcast(I32), 3: w3_scales.bitcast(I32)}

        def load_x(s, c):
            src = xT[512 * s : 512 * s + 512, 256 * c : 256 * c + 256]
            nc.sync.dma_start(raw[s, c][:], src.rearrange("(p j) w -> p j w", j=4))

        def load_words(w, e):
            dst = words[w][:, e * 2048 : (e + 1) * 2048].bitcast(I32)
            nc.sync.dma_start(dst.rearrange("p (s i) -> p s i", s=2), word_src[w][e].rearrange("s p i -> p s i"))

        def load_scales(queue, w, e0, e1):
            for q in range(4):
                dst = planes[w][32 * q : 32 * q + 4, e0 * 1024 : e1 * 1024].bitcast(I32)
                src = scale_src[w][e0:e1, :, 4 * q : 4 * q + 4, :]
                queue.dma_start(dst.rearrange("p (k i) -> p k i", i=128), src.rearrange("e s q i -> q (e s) i"))

        for s in range(2):
            for c in range(2):
                load_x(s, c)
        nc.sync.dma_start(offs_t[:], offs)
        load_words(1, 2)
        load_words(3, 2)
        load_scales(nc.sync, 1, 2, 4)
        load_scales(nc.gpsimd, 3, 2, 4)
        make_identity(nc, ident[:])
        load_words(1, 3)
        load_words(3, 3)
        nc.sync.dma_start(
            w2_t[:].bitcast(I32).rearrange("p (e i) -> p e i", e=E),
            w2_words.bitcast(I32).rearrange("e s p i -> p (e s) i"),
        )
        for q in range(4):
            dst = w2_plane[32 * q : 32 * q + 4, :].bitcast(I32)
            src = w2_scales.bitcast(I32)[:, :, 4 * q : 4 * q + 4, :]
            nc.sync.dma_start(dst.rearrange("p (k i) -> p k i", i=64), src.rearrange("e s q i -> q (e s) i"))
        load_scales(nc.sync, 1, 0, 2)
        load_scales(nc.gpsimd, 3, 0, 2)
        for e in (1, 0):
            for w in (1, 3):
                load_words(w, e)
        nc.sync.dma_start(pos1_t[:], pos1)
        nc.sync.dma_start(pos2_t[:], pos2)
        for g in range(2):
            nc.sync.dma_start(gates[g][:], gate[g, 0:128, :])

        def interleave(s, c, split):
            src = raw[s, c][:].rearrange("p j w -> p w j")
            if split > 0:
                nc.vector.tensor_copy(grouped[s, c][:, :split, :], src[:, :split, :])
            if split < 256:
                nc.scalar.activation(grouped[s, c][:, split:, :], src[:, split:, :], COPY)

        def quantise_x(s, c):
            cols = slice(256 * c, 256 * c + 256)
            nc.vector.quantize_mx(
                out=codes[s][:, cols].bitcast(E4M3), scales=bytes_[s][:, cols], in_=grouped[s, c][:].rearrange("p w j -> p (w j)")
            )

        def gather(k, s):
            e, first, count = PIECES[k]
            cols = slice(first, first + count)
            picks = offs_t[:, first // 16 : (first + count) // 16]
            nc.vector.tensor_copy(g_codes[s][:, cols], codes[s][:].indirect(picks))
            nc.vector.tensor_copy(g_bytes[s][:, cols], bytes_[s][:].indirect(picks))

        h_tiles = {}

        def layer1(k):
            e, first, count = PIECES[k]
            banks = []
            for b in range(count // 128):
                cols = slice(first + 128 * b, first + 128 * b + 128)
                pair = []
                for w in (1, 3):
                    bank = psum.tile([128, 512], F32, name=f"sum{w}")
                    for s in range(2):
                        wcol = (2 * e + s)
                        nc.tensor.matmul_mx(
                            out=bank[:],
                            lhsT=g_codes[s][:, cols].bitcast(E4M3),
                            lhsT_scale=g_bytes[s][:, cols],
                            rhs=words[w][:, wcol * 1024 : (wcol + 1) * 1024].bitcast(E2M1),
                            rhs_scale=planes[w][:, wcol * 512 : (wcol + 1) * 512],
                            start=(s == 0),
                            stop=(s == 1),
                        )
                    pair.append(bank)
                banks.append(pair)
            return banks

        def gated(k, banks):
            e, first, count = PIECES[k]
            for b in range(count // 128):
                a_bank, b_bank = banks[b]
                act = keep.tile([128, 512], F32, name=f"act{k}{b}")
                h = keep.tile([128, 512], BF16, name=f"h{k}{b}", align_bytes=64)
                order = "p (m u e) -> p u m e"
                there = "p (u m e) -> p u m e"
                nc.scalar.activation(act[:].rearrange(there, u=2, e=2), a_bank[:].rearrange(order, u=2, e=2), RELU)
                nc.vector.tensor_tensor(
                    h[:].rearrange(there, u=2, e=2), b_bank[:].rearrange(order, u=2, e=2), act[:].rearrange(there, u=2, e=2), MULT
                )
                h_tiles[k, b] = h

        turned = {}

        def turn(k):
            e, first, count = PIECES[k]
            bank = psum.tile([128, 2, count], F32, name="turn")
            for b in range(count // 128):
                for u in range(2):
                    nc.tensor.transpose(
                        bank[:, u, 128 * b : 128 * b + 128], h_tiles[k, b][:].bitcast(F32)[:, 128 * u : 128 * u + 128], ident[:]
                    )
            hT = keep.tile([128, 4 * count], BF16, name=f"hT{k}", align_bytes=64)
            nc.scalar.copy(hT[:].bitcast(F32).rearrange("p (n u) -> p n u", u=2), bank[:].rearrange("p u n -> p n u"))
            turned[k] = hT

        hq = {}

        def quantise_h(k):
            e, first, count = PIECES[k]
            hc = keep.tile([128, count], U32, name=f"hc{k}", align_bytes=64)
            hs = keep.tile([128, count], U8, name=f"hs{k}", align_bytes=64)
            nc.vector.quantize_mx(out=hc[:].bitcast(E4M3), scales=hs[:], in_=turned[k][:])
            hq[k] = (hc, hs)

        def layer2(k):
            e, first, count = PIECES[k]
            hc, hs = hq[k]
            bank = psum.tile([128, 2, count], F32, name="ybank")
            for n in range(2):
                nc.tensor.matmul_mx(
                    out=bank[:, n, :],
                    lhsT=w2_t[:, e * 512 + 256 * n : e * 512 + 256 * n + 256].bitcast(E2M1),
                    lhsT_scale=w2_plane[:, e * 256 + 128 * n : e * 256 + 128 * n + 128],
                    rhs=hc[:].bitcast(E4M3),
                    rhs_scale=hs[:],
                    start=True,
                    stop=True,
                )
            for n in range(2):
                nc.scalar.copy(y[n][:, first : first + count], bank[:, n, :])

        interleave(0, 0, 176)
        interleave(0, 1, 176)
        quantise_x(0, 0)
        quantise_x(0, 1)
        interleave(1, 0, 0)
        interleave(1, 1, 0)
        gather(0, 0)
        gather(1, 0)
        quantise_x(1, 0)
        quantise_x(1, 1)
        gather(0, 1)
        banks = {}
        banks[0] = layer1(0)
        gather(1, 1)
        gated(0, banks[0])
        banks[1] = layer1(1)
        gather(2, 0)
        gather(2, 1)
        turn(0)
        gated(1, banks[1])
        quantise_h(0)
        banks[2] = layer1(2)
        layer2(0)
        turn(1)
        gather(3, 0)
        gather(3, 1)
        gated(2, banks[2])
        quantise_h(1)
        banks[3] = layer1(3)
        layer2(1)
        turn(2)
        gather(4, 0)
        gather(4, 1)
        gated(3, banks[3])
        quantise_h(2)
        banks[4] = layer1(4)
        layer2(2)
        turn(3)
        gated(4, banks[4])
        quantise_h(3)
        turn(4)
        layer2(3)
        quantise_h(4)
        layer2(4)

        for n in range(2):
            first_term = keep.tile([128, T], F32, name=f"first{n}")
            second_term = keep.tile([128, T], F32, name=f"second{n}")
            total = keep.tile([128, T], F32, name=f"total{n}")
            nc.vector.tensor_tensor(first_term[:], y[n][:].indirect(pos1_t[:]), gates[0][:], MULT)
            nc.vector.tensor_tensor(second_term[:], y[n][:].indirect(pos2_t[:]), gates[1][:], MULT)
            for cols in ((slice(0, T),), (slice(0, T // 2), slice(T // 2, T)))[n]:
                nc.vector.tensor_tensor(total[:, cols], first_term[:, cols], second_term[:, cols], ADD)
                nc.sync.dma_start(out[128 * n : 128 * n + 128, cols], total[:, cols])
